import numpy as np
import ml_dtypes


def mxq(x, axis, fmt="e4m3"):
    dtype, down = {"e4m3": (ml_dtypes.float8_e4m3fn, 7), "e5m2": (ml_dtypes.float8_e5m2, 14)}[fmt]
    v = np.moveaxis(np.asarray(x, np.float32).astype(ml_dtypes.bfloat16).astype(np.float64), axis, -1)
    blocks = v.reshape(v.shape[:-1] + (-1, 32))
    amax = np.abs(blocks).max(-1, keepdims=True)
    byte = np.maximum(np.where(amax > 0, np.frexp(amax)[1] - 1 + 127, 0) - down, 1)
    scale = np.exp2(byte - 127.0)
    codes = (blocks / scale).astype(np.float32).astype(dtype).astype(np.float64)
    return np.moveaxis((codes * scale).reshape(v.shape), -1, axis)


WIDE = False


def mx_kscale(k):
    if not WIDE:
        return np.ones(k)
    levels = np.array([10, -10, 5, -5, 0])
    if k % 512:
        return np.exp2(np.random.permutation(np.resize(levels, k // 32))).repeat(32)
    a = np.empty((k // 512, 16))
    for p in range(k // 512):
        a[p, :8] = np.random.permutation(np.resize(levels, 8))
        for g in range(8):
            far = levels[np.abs(levels - a[p, g]) >= 10]
            a[p, g + 8] = far[np.random.randint(len(far))]
    return np.exp2(a.ravel()).repeat(32)


def f64(x):
    return np.asarray(x).astype(np.float64)


def striped(idx):
    return np.tile(idx.reshape(-1, 16).T, (8, 1)).astype(np.uint16)


def unstriped(offs):
    return offs[:16].T.reshape(-1).astype(np.int64)


def striped8(idx):
    return np.concatenate([x.reshape(-1, 16).T for x in idx]).astype(np.uint16)


def runs(offs, k):
    lists = np.stack([offs[16 * r : 16 * r + 16].T.reshape(-1) for r in range(8)]).astype(np.int64)
    return lists[np.arange(k) % 512 // 64]


def pack_weight(w):
    k, n = w.shape
    w = f64(np.asarray(w, np.float32).astype(ml_dtypes.bfloat16)).reshape(k // 32, 32, n)
    amax = np.abs(w).max(1)
    byte = np.clip(np.where(amax > 0, np.frexp(amax)[1] - 1 + 127 - 7, 1), 1, 254)
    scaled = (w * np.exp2(127.0 - byte)[:, None, :]).reshape(k, n).astype(np.float32)
    words = np.ascontiguousarray(scaled.reshape(k // 512, 128, 4, n).transpose(0, 1, 3, 2)).astype(ml_dtypes.float8_e4m3fn).view(np.uint8)
    return words, np.ascontiguousarray(byte.astype(np.uint8).reshape(k // 512, 16, n))


def unpack_weight(words, scales):
    g, p, n, _ = words.shape
    vals = np.ascontiguousarray(words).view(ml_dtypes.float8_e4m3fn).astype(np.float64) * np.repeat(np.exp2(scales.astype(np.float64) - 127.0), 8, axis=1)[..., None]
    return vals.transpose(0, 1, 3, 2).reshape(g * 512, n)


def sigmoid(v):
    return 1.0 / (1.0 + np.exp(-np.maximum(v, -700.0)))

def planes(y):
    n, m = y.shape
    v = y.astype(np.float32).astype(ml_dtypes.bfloat16).astype(np.float64).reshape(n // 32, 32, m)
    top = np.abs(v).max(1)
    byte = np.clip(np.where(top > 0, np.frexp(top)[1] - 1 + 127 - 7, 1), 1, 254)
    codes = (v * np.exp2(127.0 - byte)[:, None, :]).reshape(n, m).astype(np.float32).astype(ml_dtypes.float8_e4m3fn).view(np.uint8)
    words = codes.reshape(n // 512, 128, 4, m).transpose(0, 1, 3, 2)
    return np.ascontiguousarray(words), np.ascontiguousarray(byte.astype(np.uint8).reshape(n // 512, 16, m))


K, T, S, N, H = 512, 2048, 512, 512, 512


def setup_inputs():
    n = np.random.standard_normal
    s = mx_kscale(K)[:, None]
    u = mx_kscale(H)
    packed_xT = pack_weight(n((K, T)) * s)
    packed_w1 = pack_weight(n((K, H)) / np.sqrt(K) / s)
    packed_w2 = pack_weight(n((K, H)) / np.sqrt(K) / s)
    packed_w3 = pack_weight(n((K, H)) / np.sqrt(K) / s)
    packed_w4 = pack_weight(n((H, N)) / np.sqrt(H) / u[:, None])
    return {
        "x_words": packed_xT[0],
        "x_scales": packed_xT[1],
        "w1_words": packed_w1[0],
        "w1_scales": packed_w1[1],
        "w2_words": packed_w2[0],
        "w2_scales": packed_w2[1],
        "w3_words": packed_w3[0],
        "w3_scales": packed_w3[1],
        "gn": (np.random.uniform(0.5, 1.5, (H, 1)) * u[:, None]).astype(np.float32),
        "w4_words": packed_w4[0],
        "w4_scales": packed_w4[1],
        "offs": striped(np.random.permutation(T)[:S]),
        "two": striped(np.random.permutation(T)[:S]),
        "three": striped(np.random.permutation(T)[:S]),
        "n1": striped8(np.stack([np.random.permutation(S) for _ in range(8)])),
        "n2": striped8(np.stack([np.random.permutation(S) for _ in range(8)])),
        "n3": striped8(np.stack([np.random.permutation(S) for _ in range(8)])),
        "n4": striped8(np.stack([np.random.permutation(S) for _ in range(8)])),
        "n5": striped8(np.stack([np.random.permutation(S) for _ in range(8)])),
        "n6": striped8(np.stack([np.random.permutation(S) for _ in range(8)])),
    }


def reference(x_words, x_scales, w1_words, w1_scales, w2_words, w2_scales, w3_words, w3_scales, gn, w4_words, w4_scales, offs, two, three, n1, n2, n3, n4, n5, n6):
    xq = unpack_weight(x_words, x_scales)[:, unstriped(offs)]
    y = unpack_weight(w1_words, w1_scales).T @ xq
    x_two = unpack_weight(x_words, x_scales)[:, unstriped(two)]
    d = unpack_weight(w2_words, w2_scales).T @ x_two
    m1 = y + (sigmoid(d[np.arange(H)[:, None], runs(n2, H)] - d)) * (y[np.arange(H)[:, None], runs(n1, H)] - y)
    x_three = unpack_weight(x_words, x_scales)[:, unstriped(three)]
    b = unpack_weight(w3_words, w3_scales).T @ x_three
    z = f64(gn) * ((m1 + m1[np.arange(H)[:, None], runs(n3, H)]) * (sigmoid(b + b[np.arange(H)[:, None], runs(n4, H)])))
    h = unpack_weight(w4_words, w4_scales).T @ mxq(z, 0, "e4m3")
    pa = h[np.arange(N)[:, None], runs(n5, N)]
    pb = h[np.arange(N)[:, None], runs(n6, N)]
    mu = 0.3125 * (h + pa + pb)
    out_0 = (h - mu) / (np.sqrt((pa - mu) ** 2 + (pb - mu) ** 2 + 0.25))
    return (out_0,) + planes(out_0)

@@ -1,0 +1,263 @@
+from contextlib import ExitStack
+
+import concourse.mybir as mybir
+from concourse.masks import make_identity
+
+K, T, S, N, H = 512, 2048, 512, 512, 512
+FLOPS = 2 * S * (3 * K * H + H * N)
+
+F32 = mybir.dt.float32
+BF16 = mybir.dt.bfloat16
+I32 = mybir.dt.int32
+U32 = mybir.dt.uint32
+U16 = mybir.dt.uint16
+U8 = mybir.dt.uint8
+FP8X4 = mybir.dt.float8_e4m3fn_x4
+ADD = mybir.AluOpType.add
+SUB = mybir.AluOpType.subtract
+MULT = mybir.AluOpType.mult
+ACT = mybir.ActivationFunctionType
+
+P = 128
+PACK = 4
+BANK = 512
+LIST_COL = 16
+CHUNKS = ((0, 256), (256, 128), (384, 128))
+GROUPS = (2, 4, 2)
+
+
+def tile_picked_triopullbtriebstd_none_po_kernel(
+    tc, x_words, x_scales, w1_words, w1_scales, w2_words, w2_scales, w3_words, w3_scales, gn, w4_words, w4_scales,
+    offs, two, three, n1, n2, n3, n4, n5, n6, out_0, out_1, out_2,
+):
+    nc = tc.nc
+    with ExitStack() as ctx:
+        lists = ctx.enter_context(tc.tile_pool(name="lists", bufs=1))
+        sb = ctx.enter_context(tc.tile_pool(name="sb", bufs=1))
+        psum = ctx.enter_context(tc.psum_pool(name="psum", bufs=8))
+
+        def tile(name, shape, dtype=F32, after=""):
+            return sb.tile(shape, dtype, name=name, tag=after or name, align_bytes=64)
+
+        def bank():
+            return psum.tile([P, BANK], F32, name="bank")
+
+        def load_list(name, src):
+            dst = lists.tile([P, S // LIST_COL], U16, name=name)
+            nc.sync.dma_start(dst[:], src)
+            return dst
+
+        def load_words(name, src, width):
+            dst = tile(name, [P, width], I32)
+            nc.sync.dma_start(dst[:], src[0].rearrange("p n t -> p (n t)").bitcast(I32))
+            return dst
+
+        def zeroed_plane(name, width):
+            dst = tile(name, [P, width], U8)
+            nc.gpsimd.memset(dst[:].bitcast(I32), 0)
+            return dst
+
+        def load_scales(plane, first, src):
+            for q in range(4):
+                rows = slice(32 * q + first, 32 * q + first + 4)
+                nc.sync.dma_start(plane[rows, :].bitcast(I32), src[0, 4 * q : 4 * q + 4, :].bitcast(I32))
+
+        def deal(name, src, dtype):
+            dst = tile(name, [P, H], dtype)
+            nc.vector.tensor_copy(dst[:].rearrange("p (t m) -> p t m", t=PACK), src[:].rearrange("p (m t) -> p t m", t=PACK))
+            return dst
+
+        def pick_words(name, offsets, after=""):
+            words = tile(name, [P, S], U32, after)
+            nc.vector.tensor_copy(words[:], xw[:].bitcast(U32).indirect(offsets[:]))
+            return words
+
+        def pick_scales(name, offsets, after=""):
+            scales = tile(name, [P, S], U8, after)
+            nc.vector.tensor_copy(scales[:], xs[:].indirect(offsets[:]))
+            return scales
+
+        def product(dst, weights, plane, first, t, words, scales):
+            cols = slice(P * t, P * (t + 1))
+            nc.tensor.matmul_mx(
+                dst, lhsT=weights[:, cols].bitcast(FP8X4), lhsT_scale=plane[first:P, cols],
+                rhs=words.bitcast(FP8X4), rhs_scale=scales, start=True, stop=True,
+            )
+
+        def woven(ap):
+            return ap.rearrange("p t (c i) -> p c t i", i=4)
+
+        def woven_out(ap):
+            return ap.rearrange("p (c i t) -> p c t i", i=4, t=PACK)
+
+        xs = zeroed_plane("xs", T)
+        plane_a = zeroed_plane("plane_a", H)
+        plane_b = zeroed_plane("plane_b", H)
+        warm = tile("warm", [P, 2])
+        nc.vector.memset(warm[:, 0:1], 1.0)
+        nc.scalar.activation(warm[:, 1:2], warm[:, 0:1], ACT.Sigmoid)
+        l_three = load_list("l_three", three)
+        l_two = load_list("l_two", two)
+        l_offs = load_list("l_offs", offs)
+        l4 = load_list("l4", n4)
+        l2 = load_list("l2", n2)
+        l1 = load_list("l1", n1)
+        xw = load_words("xw", x_words, T)
+        w3_raw = load_words("w3_raw", w3_words, H)
+        load_scales(xs, 0, x_scales)
+        load_scales(plane_a, 0, w3_scales)
+        w2_raw = load_words("w2_raw", w2_words, H)
+        load_scales(plane_b, 0, w2_scales)
+        load_scales(plane_b, 4, w1_scales)
+        load_scales(plane_b, 8, w4_scales)
+        w1_raw = load_words("w1_raw", w1_words, H)
+        gain = tile("gain", [P, PACK])
+        nc.sync.dma_start(gain[:], gn.rearrange("(p t) o -> p (t o)", t=PACK))
+        l3 = load_list("l3", n3)
+        w4_raw = load_words("w4_raw", w4_words, N)
+        l5 = load_list("l5", n5)
+        l6 = load_list("l6", n6)
+        ident = tile("ident", [P, P])
+        make_identity(nc, ident[:])
+
+        low, high = slice(0, S), slice(S, 2 * S)
+        win_d = [tile("win_d%d" % t, [P, 2 * S]) for t in range(PACK)]
+        win_y = [tile("win_y%d" % t, [P, 2 * S]) for t in range(PACK)]
+        win_b = [tile("win_b%d" % t, [P, 2 * S]) for t in range(PACK)]
+        gate_1 = tile("gate_1", [P, PACK, S])
+        gate_2 = tile("gate_2", [P, PACK, S])
+        win_m = [tile("win_m%d" % t, [P, S]) for t in range(PACK)]
+        m_again = tile("m_again", [P, PACK, S])
+
+        def twice(win, weights, plane, first, words, scales):
+            for t in range(PACK):
+                acc = bank()
+                product(acc[:], weights, plane, first, t, words[:], scales[:])
+                nc.scalar.copy(win[t ^ 1][:, high], acc[:])
+                nc.scalar.copy(win[t][:, low], acc[:])
+
+        def make_y(t):
+            acc = bank()
+            product(acc[:], w1, dealt_b, 4, t, offs_words[:], offs_scales[:])
+            nc.scalar.activation(win_y[t][:, low], acc[:], ACT.Copy, scale=gain[:, t : t + 1])
+
+        def gate(name, dst, win, offsets, op, t):
+            arg = tile("%s%d" % (name, t), [P, S])
+            nc.vector.tensor_tensor(arg[:], win[t][:].indirect(offsets[:]), win[t ^ 1][:, high], op)
+            nc.scalar.activation(dst[:, t, :], arg[:], ACT.Sigmoid)
+
+        def mix(t):
+            pulled = tile("pulled%d" % t, [P, S])
+            nc.vector.scalar_tensor_tensor(win_y[t][:, high], gate_1[:, t, :], 1.0, win_y[t][:, low], SUB, MULT)
+            nc.vector.tensor_tensor(pulled[:], win_y[t][:].indirect(l1[:]), gate_1[:, t, :], MULT)
+            nc.vector.tensor_tensor(win_m[t][:], pulled[:], win_y[t][:, high], SUB)
+            nc.scalar.copy(m_again[:, t, :], win_m[t][:])
+
+        three_words = pick_words("three_words", l_three)
+        three_scales = pick_scales("three_scales", l_three)
+        two_words = pick_words("two_words", l_two)
+        w3 = deal("w3", w3_raw, I32)
+        dealt_a = deal("dealt_a", plane_a, U8)
+        twice(win_b, w3, dealt_a, 0, three_words, three_scales)
+        two_scales = pick_scales("two_scales", l_two, "plane_a")
+        w2 = deal("w2", w2_raw, I32)
+        dealt_b = deal("dealt_b", plane_b, U8)
+        twice(win_d, w2, dealt_b, 0, two_words, two_scales)
+        offs_words = pick_words("offs_words", l_offs, "w2_raw")
+        w1 = deal("w1", w1_raw, I32)
+        offs_scales = pick_scales("offs_scales", l_offs, "w1_raw")
+        for t in range(PACK):
+            gate("b_sum", gate_2, win_b, l4, ADD, t)
+        for t in range(PACK):
+            gate("d_diff", gate_1, win_d, l2, SUB, t)
+            make_y(t)
+        nc.scalar.activation(warm[:, 1:2], gate_1[:, PACK - 1, 0:1], ACT.Abs_reciprocal_sqrt, bias=0.25)
+        w4 = deal("w4", w4_raw, I32)
+        for t in range(PACK):
+            mix(t)
+
+        z_words = tile("z_words", [P, S], U32)
+        z_scales = tile("z_scales", [P, S], U8)
+        win_h = [tile("win_h%d" % t, [P, S]) for t in range(PACK)]
+        h_part = []
+        h_banks = []
+        for c, (c0, width) in enumerate(CHUNKS):
+            cols = slice(c0, c0 + width)
+            entries = slice(c0 // LIST_COL, (c0 + width) // LIST_COL)
+            m_sum = tile("m_sum%d" % c, [P, PACK, width])
+            for t in range(PACK):
+                nc.vector.tensor_tensor(m_sum[:, t, :], win_m[t][:].indirect(l3[:, entries]), m_again[:, t, cols], ADD)
+            z = tile("z%d" % c, [P, PACK * width], BF16)
+            nc.vector.tensor_tensor(woven_out(z[:]), woven(m_sum[:]), woven(gate_2[:, :, cols]), MULT)
+            nc.vector.quantize_mx(z_words[:, cols].bitcast(FP8X4), z_scales[:, cols], z[:])
+            part = tile("h_part%d" % c, [P, PACK * width])
+            h_part.append(part)
+            per_bank = BANK // width
+            for t0 in range(0, PACK, per_bank):
+                acc = bank()
+                for j in range(per_bank):
+                    product(acc[:, j * width : (j + 1) * width], w4, dealt_b, 8, t0 + j, z_words[:, cols], z_scales[:, cols])
+                for j in range(per_bank):
+                    nc.scalar.copy(win_h[t0 + j][:, cols], acc[:, j * width : (j + 1) * width])
+                h_banks.append((part[:, t0 * width : t0 * width + BANK], acc))
+        for dst, acc in h_banks:
+            nc.scalar.activation(dst, acc[:], ACT.Copy, scale=8.0 / 15.0)
+
+        def turned_sum(terms, size):
+            acc = bank()
+            for j in range(size // P):
+                block = slice(P * j, P * (j + 1))
+                for n, term in enumerate(terms):
+                    nc.tensor.matmul(
+                        acc[:, block], lhsT=term[:, block], rhs=ident[:], is_transpose=True,
+                        start=(n == 0), stop=(n == len(terms) - 1),
+                    )
+            return acc[:, 0:size]
+
+        o_words = tile("o_words", [P, S], I32)
+        o_scales = tile("o_scales", [P, S], U8)
+        out_rows = out_0.rearrange("(p t) c -> p t c", t=PACK)
+        out_words = out_1[0].rearrange("p n t -> p (n t)").bitcast(I32)
+        root_half = 0.5**0.5
+        unit = 0
+        lanes = [tile("lane%d" % n, [P, BANK]) for n in range(3)]
+        for c, (c0, width) in enumerate(CHUNKS):
+            cols = slice(c0, c0 + width)
+            entries = slice(c0 // LIST_COL, (c0 + width) // LIST_COL)
+            result = tile("result%d" % c, [P, PACK * width])
+            group = GROUPS[c]
+            size = group * width
+            for t0 in range(0, PACK, group):
+                span = slice(t0 * width, t0 * width + size)
+                name = "%d_%d" % (c, t0)
+                neg_pa = tile("neg_pa" + name, [P, size])
+                both = lanes[unit % 3][:, 0:size]
+                unit = unit + 1
+                centred = tile("centred" + name, [P, size])
+                for j in range(group):
+                    own = slice(j * width, (j + 1) * width)
+                    nc.vector.tensor_scalar(neg_pa[:, own], win_h[t0 + j][:].indirect(l5[:, entries]), -1.0, 0.0, MULT, ADD)
+                for j in range(group):
+                    own = slice(j * width, (j + 1) * width)
+                    nc.vector.tensor_tensor(both[:, own], win_h[t0 + j][:].indirect(l6[:, entries]), neg_pa[:, own], SUB)
+                nc.vector.scalar_tensor_tensor(centred[:], h_part[c][:, span], -33.0 / 8.0, both[:], MULT, ADD)
+                sq_gap = tile("sq_gap" + name, [P, size])
+                sq_sum = tile("sq_sum" + name, [P, size])
+                inv = both
+                gap = turned_sum([neg_pa[:], neg_pa[:], both[:]], size)
+                nc.scalar.activation(sq_gap[:], gap, ACT.Square, scale=root_half)
+                total = turned_sum([h_part[c][:, span], centred[:]], size)
+                nc.scalar.activation(sq_sum[:], total, ACT.Square, scale=0.375 * root_half)
+                squares = turned_sum([sq_gap[:], sq_sum[:]], size)
+                nc.scalar.activation(inv[:], squares, ACT.Abs_reciprocal_sqrt, bias=0.25)
+                nc.vector.scalar_tensor_tensor(result[:, span], centred[:], -0.3125, inv[:], MULT, MULT)
+            tiles = result[:].rearrange("p (t c) -> p t c", t=PACK)
+            nc.sync.dma_start(out_rows[:, :, cols], tiles)
+            rounded = tile("rounded%d" % c, [P, PACK * width], BF16)
+            nc.vector.tensor_copy(woven_out(rounded[:]), woven(tiles))
+            nc.vector.quantize_mx(o_words[:, cols].bitcast(FP8X4), o_scales[:, cols], rounded[:])
+            nc.sync.dma_start(out_words[:, cols], o_words[:, cols])
+            for q in range(4):
+                nc.sync.dma_start(
+                    out_2[0, 4 * q : 4 * q + 4, cols].bitcast(I32), o_scales[32 * q : 32 * q + 4, cols].bitcast(I32)
+                )

@@ -23,7 +23,8 @@ PACK = 4
 BANK = 512
 LIST_COL = 16
 CHUNKS = ((0, 256), (256, 128), (384, 128))
-GROUPS = (2, 4, 2)
+UNITS = ((0, 0, 2), (0, 2, 2), (1, 0, 4), (2, 0, 4))
+KINDS = (1, 1, 1, 0)
 
 
 def tile_picked_triopullbtriebstd_none_po_kernel(
@@ -34,7 +35,8 @@ def tile_picked_triopullbtriebstd_none_po_kernel(
     with ExitStack() as ctx:
         lists = ctx.enter_context(tc.tile_pool(name="lists", bufs=1))
         sb = ctx.enter_context(tc.tile_pool(name="sb", bufs=1))
-        psum = ctx.enter_context(tc.psum_pool(name="psum", bufs=8))
+        psum = ctx.enter_context(tc.psum_pool(name="psum", bufs=4))
+        held = ctx.enter_context(tc.psum_pool(name="held", bufs=4))
 
         def tile(name, shape, dtype=F32, after=""):
             return sb.tile(shape, dtype, name=name, tag=after or name, align_bytes=64)
@@ -64,7 +66,10 @@ def tile_picked_triopullbtriebstd_none_po_kernel(
 
         def deal(name, src, dtype):
             dst = tile(name, [P, H], dtype)
-            nc.vector.tensor_copy(dst[:].rearrange("p (t m) -> p t m", t=PACK), src[:].rearrange("p (m t) -> p t m", t=PACK))
+            run = 4 if dtype is I32 else 16
+            nc.vector.tensor_copy(
+                dst[:].rearrange("p (t c i) -> p c t i", t=PACK, i=run), src[:].rearrange("p (c i t) -> p c t i", t=PACK, i=run)
+            )
             return dst
 
         def pick_words(name, offsets, after=""):
@@ -90,29 +95,31 @@ def tile_picked_triopullbtriebstd_none_po_kernel(
         def woven_out(ap):
             return ap.rearrange("p (c i t) -> p c t i", i=4, t=PACK)
 
-        xs = zeroed_plane("xs", T)
+        xs = tile("xs", [P, T], U8)
+        nc.vector.memset(xs[:].bitcast(I32), 0)
         plane_a = zeroed_plane("plane_a", H)
         plane_b = zeroed_plane("plane_b", H)
+        plane_c = zeroed_plane("plane_c", H)
         warm = tile("warm", [P, 2])
         nc.vector.memset(warm[:, 0:1], 1.0)
         nc.scalar.activation(warm[:, 1:2], warm[:, 0:1], ACT.Sigmoid)
-        l_three = load_list("l_three", three)
         l_two = load_list("l_two", two)
         l_offs = load_list("l_offs", offs)
-        l4 = load_list("l4", n4)
-        l2 = load_list("l2", n2)
-        l1 = load_list("l1", n1)
-        xw = load_words("xw", x_words, T)
-        w3_raw = load_words("w3_raw", w3_words, H)
+        l_three = load_list("l_three", three)
         load_scales(xs, 0, x_scales)
-        load_scales(plane_a, 0, w3_scales)
-        w2_raw = load_words("w2_raw", w2_words, H)
-        load_scales(plane_b, 0, w2_scales)
-        load_scales(plane_b, 4, w1_scales)
-        load_scales(plane_b, 8, w4_scales)
-        w1_raw = load_words("w1_raw", w1_words, H)
         gain = tile("gain", [P, PACK])
         nc.sync.dma_start(gain[:], gn.rearrange("(p t) o -> p (t o)", t=PACK))
+        xw = load_words("xw", x_words, T)
+        w2_raw = load_words("w2_raw", w2_words, H)
+        load_scales(plane_a, 0, w2_scales)
+        w1_raw = load_words("w1_raw", w1_words, H)
+        l2 = load_list("l2", n2)
+        load_scales(plane_c, 0, w1_scales)
+        l1 = load_list("l1", n1)
+        load_scales(plane_b, 0, w3_scales)
+        load_scales(plane_b, 8, w4_scales)
+        l4 = load_list("l4", n4)
+        w3_raw = load_words("w3_raw", w3_words, H)
         l3 = load_list("l3", n3)
         w4_raw = load_words("w4_raw", w4_words, N)
         l5 = load_list("l5", n5)
@@ -120,71 +127,97 @@ def tile_picked_triopullbtriebstd_none_po_kernel(
         ident = tile("ident", [P, P])
         make_identity(nc, ident[:])
 
+        def turn(acc, terms, size, opens, closes):
+            blocks = [(term, slice(P * j, P * (j + 1))) for term in terms for j in range(size // P)]
+            for n, (term, block) in enumerate(blocks):
+                nc.tensor.matmul(
+                    acc[:, block], lhsT=term[:, block], rhs=ident[:], is_transpose=True,
+                    start=(opens and n == 0), stop=(closes and n == len(blocks) - 1),
+                )
+
+        def turned_sum(terms, size):
+            acc = bank()
+            turn(acc, terms, size, True, True)
+            return acc[:, 0:size]
+
         low, high = slice(0, S), slice(S, 2 * S)
         win_d = [tile("win_d%d" % t, [P, 2 * S]) for t in range(PACK)]
         win_y = [tile("win_y%d" % t, [P, 2 * S]) for t in range(PACK)]
         win_b = [tile("win_b%d" % t, [P, 2 * S]) for t in range(PACK)]
-        gate_1 = tile("gate_1", [P, PACK, S])
         gate_2 = tile("gate_2", [P, PACK, S])
         win_m = [tile("win_m%d" % t, [P, S]) for t in range(PACK)]
+        y_again = tile("y_again", [P, PACK, S])
         m_again = tile("m_again", [P, PACK, S])
 
-        def twice(win, weights, plane, first, words, scales):
-            for t in range(PACK):
-                acc = bank()
-                product(acc[:], weights, plane, first, t, words[:], scales[:])
-                nc.scalar.copy(win[t ^ 1][:, high], acc[:])
-                nc.scalar.copy(win[t][:, low], acc[:])
-
-        def make_y(t):
+        def project(window, again, weights, plane, first, words, scales, t, factor, by_dma):
             acc = bank()
-            product(acc[:], w1, dealt_b, 4, t, offs_words[:], offs_scales[:])
-            nc.scalar.activation(win_y[t][:, low], acc[:], ACT.Copy, scale=gain[:, t : t + 1])
+            product(acc[:], weights, plane, first, t, words[:], scales[:])
+            if not by_dma:
+                nc.scalar.activation(again, acc[:], ACT.Copy, scale=factor)
+            nc.scalar.activation(window, acc[:], ACT.Copy, scale=factor)
+            if by_dma:
+                nc.sync.dma_start(again, window)
 
-        def gate(name, dst, win, offsets, op, t):
+        def meet(name, win, offsets, op, t):
             arg = tile("%s%d" % (name, t), [P, S])
             nc.vector.tensor_tensor(arg[:], win[t][:].indirect(offsets[:]), win[t ^ 1][:, high], op)
-            nc.scalar.activation(dst[:, t, :], arg[:], ACT.Sigmoid)
+            return arg
 
         def mix(t):
             pulled = tile("pulled%d" % t, [P, S])
-            nc.vector.scalar_tensor_tensor(win_y[t][:, high], gate_1[:, t, :], 1.0, win_y[t][:, low], SUB, MULT)
-            nc.vector.tensor_tensor(pulled[:], win_y[t][:].indirect(l1[:]), gate_1[:, t, :], MULT)
-            nc.vector.tensor_tensor(win_m[t][:], pulled[:], win_y[t][:, high], SUB)
-            nc.scalar.copy(m_again[:, t, :], win_m[t][:])
+            nc.vector.tensor_tensor(pulled[:], win_y[t][:].indirect(l1[:]), y_again[:, t, :], SUB)
+            moved = tile("moved%d" % t, [P, S], F32, "d_diff%d" % t)
+            acc = held.tile([P, BANK], F32, name="total")
+            turn(acc, [win_y[t][:, low]], S, True, False)
+            nc.vector.tensor_tensor(moved[:], pulled[:], gate_1[:, t, :], MULT)
+            turn(acc, [moved[:]], S, False, True)
+            turned = gate_2[:, t, :]
+            nc.scalar.copy(turned[:], acc[:])
+            back = turned_sum([turned[:]], S)
+            nc.scalar.copy(win_m[t][:], back)
+            if t < 2:
+                nc.sync.dma_start(m_again[:, t, :], win_m[t][:])
+            else:
+                nc.scalar.copy(m_again[:, t, :], back)
 
-        three_words = pick_words("three_words", l_three)
+        two_scales = pick_scales("two_scales", l_two)
+        offs_scales = pick_scales("offs_scales", l_offs)
         three_scales = pick_scales("three_scales", l_three)
         two_words = pick_words("two_words", l_two)
-        w3 = deal("w3", w3_raw, I32)
-        dealt_a = deal("dealt_a", plane_a, U8)
-        twice(win_b, w3, dealt_a, 0, three_words, three_scales)
-        two_scales = pick_scales("two_scales", l_two, "plane_a")
         w2 = deal("w2", w2_raw, I32)
-        dealt_b = deal("dealt_b", plane_b, U8)
-        twice(win_d, w2, dealt_b, 0, two_words, two_scales)
-        offs_words = pick_words("offs_words", l_offs, "w2_raw")
+        dealt_a = deal("dealt_a", plane_a, U8)
+        for t in range(PACK):
+            project(win_d[t][:, low], win_d[t ^ 1][:, high], w2, dealt_a, 0, two_words, two_scales, t, 1.0, False)
+        offs_words = pick_words("offs_words", l_offs, "plane_a")
         w1 = deal("w1", w1_raw, I32)
-        offs_scales = pick_scales("offs_scales", l_offs, "w1_raw")
+        dealt_c = deal("dealt_c", plane_c, U8)
         for t in range(PACK):
-            gate("b_sum", gate_2, win_b, l4, ADD, t)
+            project(win_y[t][:, low], y_again[:, t, :], w1, dealt_c, 0, offs_words, offs_scales, t, gain[:, t : t + 1], t > 0)
+        three_words = pick_words("three_words", l_three, "w1_raw")
+        gate_1 = tile("gate_1", [P, PACK, S], F32, "plane_a")
+        w3 = deal("w3", w3_raw, I32)
+        dealt_b = deal("dealt_b", plane_b, U8)
         for t in range(PACK):
-            gate("d_diff", gate_1, win_d, l2, SUB, t)
-            make_y(t)
-        nc.scalar.activation(warm[:, 1:2], gate_1[:, PACK - 1, 0:1], ACT.Abs_reciprocal_sqrt, bias=0.25)
+            nc.vector.tensor_tensor(win_y[t][:, high], win_d[t][:].indirect(l2[:]), win_d[t ^ 1][:, high], SUB)
+            nc.scalar.activation(gate_1[:, t, :], win_y[t][:, high], ACT.Sigmoid)
+        for t in range(PACK):
+            project(win_b[t][:, low], win_b[t ^ 1][:, high], w3, dealt_b, 0, three_words, three_scales, t, 1.0, True)
         w4 = deal("w4", w4_raw, I32)
         for t in range(PACK):
             mix(t)
+        for t in range(PACK):
+            b_sum = meet("b_sum", win_b, l4, ADD, t)
+            nc.scalar.activation(gate_2[:, t, :], b_sum[:], ACT.Sigmoid)
+        nc.scalar.activation(warm[:, 1:2], gate_2[:, PACK - 1, 0:1], ACT.Abs_reciprocal_sqrt, bias=0.25)
 
         z_words = tile("z_words", [P, S], U32)
         z_scales = tile("z_scales", [P, S], U8)
         win_h = [tile("win_h%d" % t, [P, S]) for t in range(PACK)]
         h_part = []
-        h_banks = []
         for c, (c0, width) in enumerate(CHUNKS):
             cols = slice(c0, c0 + width)
             entries = slice(c0 // LIST_COL, (c0 + width) // LIST_COL)
-            m_sum = tile("m_sum%d" % c, [P, PACK, width])
+            m_sum = tile("m_sum%d" % c, [P, PACK, width], F32, ("", "m_sum0", "z0")[c])
             for t in range(PACK):
                 nc.vector.tensor_tensor(m_sum[:, t, :], win_m[t][:].indirect(l3[:, entries]), m_again[:, t, cols], ADD)
             z = tile("z%d" % c, [P, PACK * width], BF16)
@@ -199,65 +232,89 @@ def tile_picked_triopullbtriebstd_none_po_kernel(
                     product(acc[:, j * width : (j + 1) * width], w4, dealt_b, 8, t0 + j, z_words[:, cols], z_scales[:, cols])
                 for j in range(per_bank):
                     nc.scalar.copy(win_h[t0 + j][:, cols], acc[:, j * width : (j + 1) * width])
-                h_banks.append((part[:, t0 * width : t0 * width + BANK], acc))
-        for dst, acc in h_banks:
-            nc.scalar.activation(dst, acc[:], ACT.Copy, scale=8.0 / 15.0)
+                nc.scalar.activation(part[:, t0 * width : t0 * width + BANK], acc[:], ACT.Copy, scale=8.0 / 15.0)
 
-        def turned_sum(terms, size):
-            acc = bank()
-            for j in range(size // P):
-                block = slice(P * j, P * (j + 1))
-                for n, term in enumerate(terms):
-                    nc.tensor.matmul(
-                        acc[:, block], lhsT=term[:, block], rhs=ident[:], is_transpose=True,
-                        start=(n == 0), stop=(n == len(terms) - 1),
-                    )
-            return acc[:, 0:size]
+        totals = {}
+        for u, (c, t0, group) in enumerate(UNITS):
+            if KINDS[u]:
+                c0, width = CHUNKS[c]
+                totals[u] = held.tile([P, BANK], F32, name="total")
+                turn(totals[u], [h_part[c][:, t0 * width : t0 * width + BANK]], BANK, True, False)
 
         o_words = tile("o_words", [P, S], I32)
         o_scales = tile("o_scales", [P, S], U8)
         out_rows = out_0.rearrange("(p t) c -> p t c", t=PACK)
         out_words = out_1[0].rearrange("p n t -> p (n t)").bitcast(I32)
         root_half = 0.5**0.5
-        unit = 0
-        lanes = [tile("lane%d" % n, [P, BANK]) for n in range(3)]
-        for c, (c0, width) in enumerate(CHUNKS):
-            cols = slice(c0, c0 + width)
+        lanes = [tile("lane%d" % n, [P, BANK]) for n in range(4)]
+        result = [tile("result%d" % c, [P, PACK * width]) for c, (c0, width) in enumerate(CHUNKS)]
+        centred = [tile("centred%d" % u, [P, BANK]) for u in range(len(UNITS))]
+
+        def root(u):
+            c, t0, group = UNITS[u]
+            c0, width = CHUNKS[c]
             entries = slice(c0 // LIST_COL, (c0 + width) // LIST_COL)
-            result = tile("result%d" % c, [P, PACK * width])
-            group = GROUPS[c]
-            size = group * width
-            for t0 in range(0, PACK, group):
-                span = slice(t0 * width, t0 * width + size)
-                name = "%d_%d" % (c, t0)
-                neg_pa = tile("neg_pa" + name, [P, size])
-                both = lanes[unit % 3][:, 0:size]
-                unit = unit + 1
-                centred = tile("centred" + name, [P, size])
-                for j in range(group):
-                    own = slice(j * width, (j + 1) * width)
-                    nc.vector.tensor_scalar(neg_pa[:, own], win_h[t0 + j][:].indirect(l5[:, entries]), -1.0, 0.0, MULT, ADD)
-                for j in range(group):
-                    own = slice(j * width, (j + 1) * width)
-                    nc.vector.tensor_tensor(both[:, own], win_h[t0 + j][:].indirect(l6[:, entries]), neg_pa[:, own], SUB)
-                nc.vector.scalar_tensor_tensor(centred[:], h_part[c][:, span], -33.0 / 8.0, both[:], MULT, ADD)
-                sq_gap = tile("sq_gap" + name, [P, size])
-                sq_sum = tile("sq_sum" + name, [P, size])
-                inv = both
-                gap = turned_sum([neg_pa[:], neg_pa[:], both[:]], size)
+            part = h_part[c][:, t0 * width : t0 * width + BANK]
+            neg_pa = tile("neg_pa%d" % u, [P, BANK], F32, "")
+            both = lanes[(0, 1, 2, 3)[u]]
+            for j in range(group):
+                own = slice(j * width, (j + 1) * width)
+                nc.vector.tensor_scalar(neg_pa[:, own], win_h[t0 + j][:].indirect(l5[:, entries]), -1.0, 0.0, MULT, ADD)
+            for j in range(group):
+                own = slice(j * width, (j + 1) * width)
+                nc.vector.tensor_tensor(both[:, own], win_h[t0 + j][:].indirect(l6[:, entries]), neg_pa[:, own], SUB)
+            if KINDS[u] == 0:
+                pair = tile("pair", [P, 2, BANK], F32, "d_diff1")
+                sq_gap, sq_sum = pair[:, 0, :], pair[:, 1, :]
+                diff = tile("diff%d" % u, [P, BANK])
+                total = tile("total%d" % u, [P, BANK])
+                added = tile("added%d" % u, [P, BANK])
+                nc.vector.scalar_tensor_tensor(diff[:], neg_pa[:], 2.0, both[:], MULT, ADD)
+                nc.scalar.activation(sq_gap[:], diff[:], ACT.Square, scale=root_half)
+                nc.vector.scalar_tensor_tensor(total[:], part, -25.0 / 8.0, both[:], MULT, ADD)
+                nc.scalar.activation(sq_sum[:], total[:], ACT.Square, scale=0.375 * root_half)
+                nc.vector.scalar_tensor_tensor(centred[u][:], part, -33.0 / 8.0, both[:], MULT, ADD)
+                nc.vector.tensor_tensor(added[:], sq_sum[:], sq_gap[:], ADD)
+                squares = added[:]
+            else:
+                sq_gap = tile("sq_gap%d" % u, [P, BANK], F32, "b_sum%d" % u)
+                sq_sum = tile("sq_sum%d" % u, [P, BANK], F32, "d_diff%d" % u)
+                nc.vector.scalar_tensor_tensor(centred[u][:], part, -33.0 / 8.0, both[:], MULT, ADD)
+                if KINDS[u] == 1:
+                    gap = turned_sum([neg_pa[:], neg_pa[:], both[:]], BANK)
+                else:
+                    diff = tile("diff%d" % u, [P, BANK])
+                    nc.vector.scalar_tensor_tensor(diff[:], neg_pa[:], 2.0, both[:], MULT, ADD)
+                    gap = turned_sum([diff[:]], BANK)
                 nc.scalar.activation(sq_gap[:], gap, ACT.Square, scale=root_half)
-                total = turned_sum([h_part[c][:, span], centred[:]], size)
-                nc.scalar.activation(sq_sum[:], total, ACT.Square, scale=0.375 * root_half)
-                squares = turned_sum([sq_gap[:], sq_sum[:]], size)
-                nc.scalar.activation(inv[:], squares, ACT.Abs_reciprocal_sqrt, bias=0.25)
-                nc.vector.scalar_tensor_tensor(result[:, span], centred[:], -0.3125, inv[:], MULT, MULT)
-            tiles = result[:].rearrange("p (t c) -> p t c", t=PACK)
+                turn(totals[u], [centred[u][:]], BANK, False, True)
+                nc.scalar.activation(sq_sum[:], totals[u][:], ACT.Square, scale=0.375 * root_half)
+                squares = turned_sum([sq_gap[:], sq_sum[:]], BANK)
+            nc.scalar.activation(both[:], squares, ACT.Abs_reciprocal_sqrt, bias=0.25)
+
+        def finish(u):
+            c, t0, group = UNITS[u]
+            c0, width = CHUNKS[c]
+            cols = slice(c0, c0 + width)
+            nc.vector.scalar_tensor_tensor(
+                result[c][:, t0 * width : t0 * width + BANK], centred[u][:], -0.3125, lanes[(0, 1, 2, 3)[u]][:], MULT, MULT
+            )
+            if t0 + group < PACK:
+                return
+            tiles = result[c][:].rearrange("p (t c) -> p t c", t=PACK)
             nc.sync.dma_start(out_rows[:, :, cols], tiles)
-            rounded = tile("rounded%d" % c, [P, PACK * width], BF16)
-            nc.vector.tensor_copy(woven_out(rounded[:]), woven(tiles))
+            rounded = tile("rounded%d" % c, [P, PACK * width], BF16, "")
+            if "VVV"[c] == "S":
+                nc.scalar.copy(woven_out(rounded[:]), woven(tiles))
+            else:
+                nc.vector.tensor_copy(woven_out(rounded[:]), woven(tiles))
             nc.vector.quantize_mx(o_words[:, cols].bitcast(FP8X4), o_scales[:, cols], rounded[:])
             nc.sync.dma_start(out_words[:, cols], o_words[:, cols])
-            for q in range(4):
-                nc.sync.dma_start(
-                    out_2[0, 4 * q : 4 * q + 4, cols].bitcast(I32), o_scales[32 * q : 32 * q + 4, cols].bitcast(I32)
-                )
+
+        for u in range(len(UNITS) + 1):
+            if u < len(UNITS):
+                root(u)
+            if u >= 1:
+                finish(u - 1)
+        for q in range(4):
+            nc.sync.dma_start(out_2[0, 4 * q : 4 * q + 4, :].bitcast(I32), o_scales[32 * q : 32 * q + 4, :].bitcast(I32))

@@ -20,11 +20,17 @@ ACT = mybir.ActivationFunctionType
 
 P = 128
 PACK = 4
+QUADRANTS = 4
 BANK = 512
 LIST_COL = 16
-CHUNKS = ((0, 256), (256, 128), (384, 128))
-UNITS = ((0, 0, 2), (0, 2, 2), (1, 0, 4), (2, 0, 4))
-KINDS = (1, 1, 1, 0)
+LINE = 16
+HALF = S // 2
+PAIR = BANK // HALF
+UNITS = S * PACK // BANK
+TURNED_UNITS = UNITS - 1
+W4_ROWS = 4
+H_PART = 8.0 / 15.0
+ROOT_HALF = 0.5**0.5
 
 
 def tile_picked_triopullbtriebstd_none_po_kernel(
@@ -41,9 +47,6 @@ def tile_picked_triopullbtriebstd_none_po_kernel(
         def tile(name, shape, dtype=F32, after=""):
             return sb.tile(shape, dtype, name=name, tag=after or name, align_bytes=64)
 
-        def bank():
-            return psum.tile([P, BANK], F32, name="bank")
-
         def load_list(name, src):
             dst = lists.tile([P, S // LIST_COL], U16, name=name)
             nc.sync.dma_start(dst[:], src)
@@ -54,19 +57,19 @@ def tile_picked_triopullbtriebstd_none_po_kernel(
             nc.sync.dma_start(dst[:], src[0].rearrange("p n t -> p (n t)").bitcast(I32))
             return dst
 
-        def zeroed_plane(name, width):
+        def zeroed_plane(name, width, engine):
             dst = tile(name, [P, width], U8)
-            nc.gpsimd.memset(dst[:].bitcast(I32), 0)
+            engine.memset(dst[:].bitcast(I32), 0)
             return dst
 
         def load_scales(plane, first, src):
-            for q in range(4):
+            for q in range(QUADRANTS):
                 rows = slice(32 * q + first, 32 * q + first + 4)
                 nc.sync.dma_start(plane[rows, :].bitcast(I32), src[0, 4 * q : 4 * q + 4, :].bitcast(I32))
 
-        def deal(name, src, dtype):
+        def deal(name, src, dtype, item_size):
             dst = tile(name, [P, H], dtype)
-            run = 4 if dtype is I32 else 16
+            run = LINE // item_size
             nc.vector.tensor_copy(
                 dst[:].rearrange("p (t c i) -> p c t i", t=PACK, i=run), src[:].rearrange("p (c i t) -> p c t i", t=PACK, i=run)
             )
@@ -77,8 +80,8 @@ def tile_picked_triopullbtriebstd_none_po_kernel(
             nc.vector.tensor_copy(words[:], xw[:].bitcast(U32).indirect(offsets[:]))
             return words
 
-        def pick_scales(name, offsets, after=""):
-            scales = tile(name, [P, S], U8, after)
+        def pick_scales(name, offsets):
+            scales = tile(name, [P, S], U8)
             nc.vector.tensor_copy(scales[:], xs[:].indirect(offsets[:]))
             return scales
 
@@ -89,20 +92,29 @@ def tile_picked_triopullbtriebstd_none_po_kernel(
                 rhs=words.bitcast(FP8X4), rhs_scale=scales, start=True, stop=True,
             )
 
-        def woven(ap):
+        def by_tile(ap):
             return ap.rearrange("p t (c i) -> p c t i", i=4)
 
-        def woven_out(ap):
+        def by_word(ap):
             return ap.rearrange("p (c i t) -> p c t i", i=4, t=PACK)
 
-        xs = tile("xs", [P, T], U8)
-        nc.vector.memset(xs[:].bitcast(I32), 0)
-        plane_a = zeroed_plane("plane_a", H)
-        plane_b = zeroed_plane("plane_b", H)
-        plane_c = zeroed_plane("plane_c", H)
-        warm = tile("warm", [P, 2])
-        nc.vector.memset(warm[:, 0:1], 1.0)
-        nc.scalar.activation(warm[:, 1:2], warm[:, 0:1], ACT.Sigmoid)
+        def turn(acc, terms, opens, closes):
+            blocks = [(term, slice(P * j, P * (j + 1))) for term in terms for j in range(BANK // P)]
+            for n, (term, block) in enumerate(blocks):
+                nc.tensor.matmul(
+                    acc[:, block], lhsT=term[:, block], rhs=ident[:], is_transpose=True,
+                    start=(opens and n == 0), stop=(closes and n == len(blocks) - 1),
+                )
+
+        def turned_sum(terms):
+            acc = psum.tile([P, BANK], F32, name="bank")
+            turn(acc, terms, True, True)
+            return acc
+
+        xs = zeroed_plane("xs", T, nc.vector)
+        plane_w2 = zeroed_plane("plane_w2", H, nc.gpsimd)
+        plane_w34 = zeroed_plane("plane_w34", H, nc.gpsimd)
+        plane_w1 = zeroed_plane("plane_w1", H, nc.gpsimd)
         l_two = load_list("l_two", two)
         l_offs = load_list("l_offs", offs)
         l_three = load_list("l_three", three)
@@ -111,13 +123,13 @@ def tile_picked_triopullbtriebstd_none_po_kernel(
         nc.sync.dma_start(gain[:], gn.rearrange("(p t) o -> p (t o)", t=PACK))
         xw = load_words("xw", x_words, T)
         w2_raw = load_words("w2_raw", w2_words, H)
-        load_scales(plane_a, 0, w2_scales)
+        load_scales(plane_w2, 0, w2_scales)
         w1_raw = load_words("w1_raw", w1_words, H)
         l2 = load_list("l2", n2)
-        load_scales(plane_c, 0, w1_scales)
+        load_scales(plane_w1, 0, w1_scales)
         l1 = load_list("l1", n1)
-        load_scales(plane_b, 0, w3_scales)
-        load_scales(plane_b, 8, w4_scales)
+        load_scales(plane_w34, 0, w3_scales)
+        load_scales(plane_w34, W4_ROWS, w4_scales)
         l4 = load_list("l4", n4)
         w3_raw = load_words("w3_raw", w3_words, H)
         l3 = load_list("l3", n3)
@@ -126,19 +138,6 @@ def tile_picked_triopullbtriebstd_none_po_kernel(
         l6 = load_list("l6", n6)
         ident = tile("ident", [P, P])
         make_identity(nc, ident[:])
-
-        def turn(acc, terms, size, opens, closes):
-            blocks = [(term, slice(P * j, P * (j + 1))) for term in terms for j in range(size // P)]
-            for n, (term, block) in enumerate(blocks):
-                nc.tensor.matmul(
-                    acc[:, block], lhsT=term[:, block], rhs=ident[:], is_transpose=True,
-                    start=(opens and n == 0), stop=(closes and n == len(blocks) - 1),
-                )
-
-        def turned_sum(terms, size):
-            acc = bank()
-            turn(acc, terms, size, True, True)
-            return acc[:, 0:size]
 
         low, high = slice(0, S), slice(S, 2 * S)
         win_d = [tile("win_d%d" % t, [P, 2 * S]) for t in range(PACK)]
@@ -149,172 +148,151 @@ def tile_picked_triopullbtriebstd_none_po_kernel(
         y_again = tile("y_again", [P, PACK, S])
         m_again = tile("m_again", [P, PACK, S])
 
-        def project(window, again, weights, plane, first, words, scales, t, factor, by_dma):
-            acc = bank()
-            product(acc[:], weights, plane, first, t, words[:], scales[:])
+        def project(window, again, weights, plane, words, scales, t, factor, by_dma):
+            acc = psum.tile([P, BANK], F32, name="bank")
+            product(acc[:], weights, plane, 0, t, words[:], scales[:])
             if not by_dma:
                 nc.scalar.activation(again, acc[:], ACT.Copy, scale=factor)
             nc.scalar.activation(window, acc[:], ACT.Copy, scale=factor)
             if by_dma:
                 nc.sync.dma_start(again, window)
 
-        def meet(name, win, offsets, op, t):
-            arg = tile("%s%d" % (name, t), [P, S])
-            nc.vector.tensor_tensor(arg[:], win[t][:].indirect(offsets[:]), win[t ^ 1][:, high], op)
-            return arg
-
         def mix(t):
             pulled = tile("pulled%d" % t, [P, S])
             nc.vector.tensor_tensor(pulled[:], win_y[t][:].indirect(l1[:]), y_again[:, t, :], SUB)
-            moved = tile("moved%d" % t, [P, S], F32, "d_diff%d" % t)
-            acc = held.tile([P, BANK], F32, name="total")
-            turn(acc, [win_y[t][:, low]], S, True, False)
+            moved = tile("moved%d" % t, [P, S])
+            acc = held.tile([P, BANK], F32, name="held_bank")
+            turn(acc, [win_y[t][:, low]], True, False)
             nc.vector.tensor_tensor(moved[:], pulled[:], gate_1[:, t, :], MULT)
-            turn(acc, [moved[:]], S, False, True)
-            turned = gate_2[:, t, :]
-            nc.scalar.copy(turned[:], acc[:])
-            back = turned_sum([turned[:]], S)
-            nc.scalar.copy(win_m[t][:], back)
-            if t < 2:
+            turn(acc, [moved[:]], False, True)
+            nc.scalar.copy(gate_2[:, t, :], acc[:])
+            back = turned_sum([gate_2[:, t, :]])
+            nc.scalar.copy(win_m[t][:], back[:])
+            if t < PACK // 2:
                 nc.sync.dma_start(m_again[:, t, :], win_m[t][:])
             else:
-                nc.scalar.copy(m_again[:, t, :], back)
+                nc.scalar.copy(m_again[:, t, :], back[:])
 
         two_scales = pick_scales("two_scales", l_two)
         offs_scales = pick_scales("offs_scales", l_offs)
         three_scales = pick_scales("three_scales", l_three)
         two_words = pick_words("two_words", l_two)
-        w2 = deal("w2", w2_raw, I32)
-        dealt_a = deal("dealt_a", plane_a, U8)
+        w2 = deal("w2", w2_raw, I32, 4)
+        scales_w2 = deal("scales_w2", plane_w2, U8, 1)
         for t in range(PACK):
-            project(win_d[t][:, low], win_d[t ^ 1][:, high], w2, dealt_a, 0, two_words, two_scales, t, 1.0, False)
-        offs_words = pick_words("offs_words", l_offs, "plane_a")
-        w1 = deal("w1", w1_raw, I32)
-        dealt_c = deal("dealt_c", plane_c, U8)
+            project(win_d[t][:, low], win_d[t ^ 1][:, high], w2, scales_w2, two_words, two_scales, t, 1.0, False)
+        offs_words = pick_words("offs_words", l_offs, "plane_w2")
+        w1 = deal("w1", w1_raw, I32, 4)
+        scales_w1 = deal("scales_w1", plane_w1, U8, 1)
         for t in range(PACK):
-            project(win_y[t][:, low], y_again[:, t, :], w1, dealt_c, 0, offs_words, offs_scales, t, gain[:, t : t + 1], t > 0)
+            project(win_y[t][:, low], y_again[:, t, :], w1, scales_w1, offs_words, offs_scales, t, gain[:, t : t + 1], t > 0)
         three_words = pick_words("three_words", l_three, "w1_raw")
-        gate_1 = tile("gate_1", [P, PACK, S], F32, "plane_a")
-        w3 = deal("w3", w3_raw, I32)
-        dealt_b = deal("dealt_b", plane_b, U8)
+        gate_1 = tile("gate_1", [P, PACK, S], F32, "plane_w2")
+        w3 = deal("w3", w3_raw, I32, 4)
+        scales_w34 = deal("scales_w34", plane_w34, U8, 1)
         for t in range(PACK):
             nc.vector.tensor_tensor(win_y[t][:, high], win_d[t][:].indirect(l2[:]), win_d[t ^ 1][:, high], SUB)
             nc.scalar.activation(gate_1[:, t, :], win_y[t][:, high], ACT.Sigmoid)
         for t in range(PACK):
-            project(win_b[t][:, low], win_b[t ^ 1][:, high], w3, dealt_b, 0, three_words, three_scales, t, 1.0, True)
-        w4 = deal("w4", w4_raw, I32)
+            project(win_b[t][:, low], win_b[t ^ 1][:, high], w3, scales_w34, three_words, three_scales, t, 1.0, True)
+        w4 = deal("w4", w4_raw, I32, 4)
         for t in range(PACK):
             mix(t)
         for t in range(PACK):
-            b_sum = meet("b_sum", win_b, l4, ADD, t)
+            b_sum = tile("b_sum%d" % t, [P, S])
+            nc.vector.tensor_tensor(b_sum[:], win_b[t][:].indirect(l4[:]), win_b[t ^ 1][:, high], ADD)
             nc.scalar.activation(gate_2[:, t, :], b_sum[:], ACT.Sigmoid)
-        nc.scalar.activation(warm[:, 1:2], gate_2[:, PACK - 1, 0:1], ACT.Abs_reciprocal_sqrt, bias=0.25)
 
         z_words = tile("z_words", [P, S], U32)
         z_scales = tile("z_scales", [P, S], U8)
         win_h = [tile("win_h%d" % t, [P, S]) for t in range(PACK)]
-        h_part = []
-        for c, (c0, width) in enumerate(CHUNKS):
-            cols = slice(c0, c0 + width)
-            entries = slice(c0 // LIST_COL, (c0 + width) // LIST_COL)
-            m_sum = tile("m_sum%d" % c, [P, PACK, width], F32, ("", "m_sum0", "z0")[c])
+        h_banks = []
+        for half in range(2):
+            cols = slice(HALF * half, HALF * (half + 1))
+            entries = slice(cols.start // LIST_COL, cols.stop // LIST_COL)
+            m_sum = tile("m_sum%d" % half, [P, PACK, HALF], F32, "m_sum")
             for t in range(PACK):
                 nc.vector.tensor_tensor(m_sum[:, t, :], win_m[t][:].indirect(l3[:, entries]), m_again[:, t, cols], ADD)
-            z = tile("z%d" % c, [P, PACK * width], BF16)
-            nc.vector.tensor_tensor(woven_out(z[:]), woven(m_sum[:]), woven(gate_2[:, :, cols]), MULT)
+            z = tile("z%d" % half, [P, PACK * HALF], BF16)
+            if half == 0:
+                z_tiles = tile("z_tiles", [P, PACK, HALF], BF16)
+                nc.vector.tensor_tensor(z_tiles[:], m_sum[:], gate_2[:, :, cols], MULT)
+                nc.scalar.copy(by_word(z[:]), by_tile(z_tiles[:]))
+            else:
+                nc.vector.tensor_tensor(by_word(z[:]), by_tile(m_sum[:]), by_tile(gate_2[:, :, cols]), MULT)
             nc.vector.quantize_mx(z_words[:, cols].bitcast(FP8X4), z_scales[:, cols], z[:])
-            part = tile("h_part%d" % c, [P, PACK * width])
-            h_part.append(part)
-            per_bank = BANK // width
-            for t0 in range(0, PACK, per_bank):
-                acc = bank()
-                for j in range(per_bank):
-                    product(acc[:, j * width : (j + 1) * width], w4, dealt_b, 8, t0 + j, z_words[:, cols], z_scales[:, cols])
-                for j in range(per_bank):
-                    nc.scalar.copy(win_h[t0 + j][:, cols], acc[:, j * width : (j + 1) * width])
-                nc.scalar.activation(part[:, t0 * width : t0 * width + BANK], acc[:], ACT.Copy, scale=8.0 / 15.0)
-
-        totals = {}
-        for u, (c, t0, group) in enumerate(UNITS):
-            if KINDS[u]:
-                c0, width = CHUNKS[c]
-                totals[u] = held.tile([P, BANK], F32, name="total")
-                turn(totals[u], [h_part[c][:, t0 * width : t0 * width + BANK]], BANK, True, False)
+            for t0 in range(0, PACK, PAIR):
+                acc = psum.tile([P, BANK], F32, name="bank")
+                for j in range(PAIR):
+                    product(acc[:, j * HALF : (j + 1) * HALF], w4, scales_w34, W4_ROWS, t0 + j, z_words[:, cols], z_scales[:, cols])
+                for j in range(PAIR):
+                    nc.scalar.copy(win_h[t0 + j][:, cols], acc[:, j * HALF : (j + 1) * HALF])
+                h_banks.append(acc)
+        h_part = tile("h_part", [P, UNITS, BANK])
+        for u in range(UNITS):
+            nc.scalar.activation(h_part[:, u, :], h_banks[u][:], ACT.Copy, scale=H_PART)
+        totals = [held.tile([P, BANK], F32, name="held_bank") for u in range(TURNED_UNITS)]
+        for u in range(TURNED_UNITS):
+            turn(totals[u], [h_part[:, u, :]], True, False)
 
         o_words = tile("o_words", [P, S], I32)
         o_scales = tile("o_scales", [P, S], U8)
         out_rows = out_0.rearrange("(p t) c -> p t c", t=PACK)
         out_words = out_1[0].rearrange("p n t -> p (n t)").bitcast(I32)
-        root_half = 0.5**0.5
-        lanes = [tile("lane%d" % n, [P, BANK]) for n in range(4)]
-        result = [tile("result%d" % c, [P, PACK * width]) for c, (c0, width) in enumerate(CHUNKS)]
-        centred = [tile("centred%d" % u, [P, BANK]) for u in range(len(UNITS))]
+        inv_root = [tile("inv_root%d" % u, [P, BANK]) for u in range(UNITS)]
+        centred = [tile("centred%d" % u, [P, BANK]) for u in range(UNITS)]
+        result = tile("result", [P, UNITS, BANK])
 
-        def root(u):
-            c, t0, group = UNITS[u]
-            c0, width = CHUNKS[c]
-            entries = slice(c0 // LIST_COL, (c0 + width) // LIST_COL)
-            part = h_part[c][:, t0 * width : t0 * width + BANK]
-            neg_pa = tile("neg_pa%d" % u, [P, BANK], F32, "")
-            both = lanes[(0, 1, 2, 3)[u]]
-            for j in range(group):
-                own = slice(j * width, (j + 1) * width)
+        def spread(u):
+            half, t0 = u // PAIR, PAIR * (u % PAIR)
+            entries = slice(HALF * half // LIST_COL, HALF * (half + 1) // LIST_COL)
+            neg_pa = tile("neg_pa%d" % u, [P, BANK])
+            q = tile("q%d" % u, [P, BANK])
+            for j in range(PAIR):
+                own = slice(j * HALF, (j + 1) * HALF)
                 nc.vector.tensor_scalar(neg_pa[:, own], win_h[t0 + j][:].indirect(l5[:, entries]), -1.0, 0.0, MULT, ADD)
-            for j in range(group):
-                own = slice(j * width, (j + 1) * width)
-                nc.vector.tensor_tensor(both[:, own], win_h[t0 + j][:].indirect(l6[:, entries]), neg_pa[:, own], SUB)
-            if KINDS[u] == 0:
-                pair = tile("pair", [P, 2, BANK], F32, "d_diff1")
-                sq_gap, sq_sum = pair[:, 0, :], pair[:, 1, :]
-                diff = tile("diff%d" % u, [P, BANK])
-                total = tile("total%d" % u, [P, BANK])
-                added = tile("added%d" % u, [P, BANK])
-                nc.vector.scalar_tensor_tensor(diff[:], neg_pa[:], 2.0, both[:], MULT, ADD)
-                nc.scalar.activation(sq_gap[:], diff[:], ACT.Square, scale=root_half)
-                nc.vector.scalar_tensor_tensor(total[:], part, -25.0 / 8.0, both[:], MULT, ADD)
-                nc.scalar.activation(sq_sum[:], total[:], ACT.Square, scale=0.375 * root_half)
-                nc.vector.scalar_tensor_tensor(centred[u][:], part, -33.0 / 8.0, both[:], MULT, ADD)
-                nc.vector.tensor_tensor(added[:], sq_sum[:], sq_gap[:], ADD)
-                squares = added[:]
-            else:
+            for j in range(PAIR):
+                own = slice(j * HALF, (j + 1) * HALF)
+                nc.vector.tensor_tensor(q[:, own], win_h[t0 + j][:].indirect(l6[:, entries]), neg_pa[:, own], SUB)
+            if u < TURNED_UNITS:
                 sq_gap = tile("sq_gap%d" % u, [P, BANK], F32, "b_sum%d" % u)
-                sq_sum = tile("sq_sum%d" % u, [P, BANK], F32, "d_diff%d" % u)
-                nc.vector.scalar_tensor_tensor(centred[u][:], part, -33.0 / 8.0, both[:], MULT, ADD)
-                if KINDS[u] == 1:
-                    gap = turned_sum([neg_pa[:], neg_pa[:], both[:]], BANK)
-                else:
-                    diff = tile("diff%d" % u, [P, BANK])
-                    nc.vector.scalar_tensor_tensor(diff[:], neg_pa[:], 2.0, both[:], MULT, ADD)
-                    gap = turned_sum([diff[:]], BANK)
-                nc.scalar.activation(sq_gap[:], gap, ACT.Square, scale=root_half)
-                turn(totals[u], [centred[u][:]], BANK, False, True)
-                nc.scalar.activation(sq_sum[:], totals[u][:], ACT.Square, scale=0.375 * root_half)
-                squares = turned_sum([sq_gap[:], sq_sum[:]], BANK)
-            nc.scalar.activation(both[:], squares, ACT.Abs_reciprocal_sqrt, bias=0.25)
+                sq_total = tile("sq_total%d" % u, [P, BANK], F32, "moved%d" % u)
+                nc.vector.scalar_tensor_tensor(centred[u][:], h_part[:, u, :], -2.2 / H_PART, q[:], MULT, ADD)
+                gap = turned_sum([neg_pa[:], neg_pa[:], q[:]])
+                nc.scalar.activation(sq_gap[:], gap[:], ACT.Square, scale=ROOT_HALF)
+                turn(totals[u], [centred[u][:]], False, True)
+                nc.scalar.activation(sq_total[:], totals[u][:], ACT.Square, scale=0.375 * ROOT_HALF)
+                squares = turned_sum([sq_gap[:], sq_total[:]])
+            else:
+                sq_both = tile("sq_both", [P, 2, BANK], F32, "moved1")
+                gap = tile("gap", [P, BANK])
+                total = tile("total", [P, BANK])
+                squares = tile("squares", [P, BANK])
+                nc.vector.scalar_tensor_tensor(gap[:], neg_pa[:], 2.0, q[:], MULT, ADD)
+                nc.scalar.activation(sq_both[:, 0, :], gap[:], ACT.Square, scale=ROOT_HALF)
+                nc.vector.scalar_tensor_tensor(total[:], h_part[:, u, :], -5.0 / 3.0 / H_PART, q[:], MULT, ADD)
+                nc.scalar.activation(sq_both[:, 1, :], total[:], ACT.Square, scale=0.375 * ROOT_HALF)
+                nc.vector.scalar_tensor_tensor(centred[u][:], h_part[:, u, :], -2.2 / H_PART, q[:], MULT, ADD)
+                nc.vector.tensor_tensor(squares[:], sq_both[:, 1, :], sq_both[:, 0, :], ADD)
+            nc.scalar.activation(inv_root[u][:], squares[:], ACT.Abs_reciprocal_sqrt, bias=0.25)
 
         def finish(u):
-            c, t0, group = UNITS[u]
-            c0, width = CHUNKS[c]
-            cols = slice(c0, c0 + width)
-            nc.vector.scalar_tensor_tensor(
-                result[c][:, t0 * width : t0 * width + BANK], centred[u][:], -0.3125, lanes[(0, 1, 2, 3)[u]][:], MULT, MULT
-            )
-            if t0 + group < PACK:
-                return
-            tiles = result[c][:].rearrange("p (t c) -> p t c", t=PACK)
-            nc.sync.dma_start(out_rows[:, :, cols], tiles)
-            rounded = tile("rounded%d" % c, [P, PACK * width], BF16, "")
-            if "VVV"[c] == "S":
-                nc.scalar.copy(woven_out(rounded[:]), woven(tiles))
-            else:
-                nc.vector.tensor_copy(woven_out(rounded[:]), woven(tiles))
-            nc.vector.quantize_mx(o_words[:, cols].bitcast(FP8X4), o_scales[:, cols], rounded[:])
-            nc.sync.dma_start(out_words[:, cols], o_words[:, cols])
+            nc.vector.scalar_tensor_tensor(result[:, u, :], centred[u][:], -0.3125, inv_root[u][:], MULT, MULT)
+            if u % PAIR == PAIR - 1:
+                half = u // PAIR
+                cols = slice(HALF * half, HALF * (half + 1))
+                tiles = result[:, PAIR * half : PAIR * (half + 1), :].rearrange("p u (j c) -> p (u j) c", j=PAIR)
+                nc.sync.dma_start(out_rows[:, :, cols], tiles)
+                rounded = tile("rounded%d" % half, [P, PACK * HALF], BF16)
+                nc.vector.tensor_copy(by_word(rounded[:]), by_tile(tiles))
+                nc.vector.quantize_mx(o_words[:, cols].bitcast(FP8X4), o_scales[:, cols], rounded[:])
+                nc.sync.dma_start(out_words[:, cols], o_words[:, cols])
 
-        for u in range(len(UNITS) + 1):
-            if u < len(UNITS):
-                root(u)
-            if u >= 1:
-                finish(u - 1)
-        for q in range(4):
-            nc.sync.dma_start(out_2[0, 4 * q : 4 * q + 4, :].bitcast(I32), o_scales[32 * q : 32 * q + 4, :].bitcast(I32))
+        spread(0)
+        for u in range(1, UNITS):
+            spread(u)
+            finish(u - 1)
+        finish(UNITS - 1)
+        for r in range(QUADRANTS):
+            queue = (nc.scalar, nc.sync)[r % 2]
+            queue.dma_start(out_2[0, 4 * r : 4 * r + 4, :].bitcast(I32), o_scales[32 * r : 32 * r + 4, :].bitcast(I32))

@@ -29,7 +29,8 @@ PAIR = BANK // HALF
 UNITS = S * PACK // BANK
 TURNED_UNITS = UNITS - 1
 W4_ROWS = 4
-H_PART = 8.0 / 15.0
+H_LESS = -11.0 / 5.0
+H_MORE = 8.0 / 15.0
 ROOT_HALF = 0.5**0.5
 
 
@@ -115,6 +116,9 @@ def tile_picked_triopullbtriebstd_none_po_kernel(
         plane_w2 = zeroed_plane("plane_w2", H, nc.gpsimd)
         plane_w34 = zeroed_plane("plane_w34", H, nc.gpsimd)
         plane_w1 = zeroed_plane("plane_w1", H, nc.gpsimd)
+        warm = tile("warm", [P, 2])
+        nc.vector.memset(warm[:, 0:1], 1.0)
+        nc.scalar.activation(warm[:, 1:2], warm[:, 0:1], ACT.Sigmoid)
         l_two = load_list("l_two", two)
         l_offs = load_list("l_offs", offs)
         l_three = load_list("l_three", three)
@@ -202,6 +206,7 @@ def tile_picked_triopullbtriebstd_none_po_kernel(
             b_sum = tile("b_sum%d" % t, [P, S])
             nc.vector.tensor_tensor(b_sum[:], win_b[t][:].indirect(l4[:]), win_b[t ^ 1][:, high], ADD)
             nc.scalar.activation(gate_2[:, t, :], b_sum[:], ACT.Sigmoid)
+        nc.scalar.activation(warm[:, 1:2], gate_2[:, PACK - 1, 0:1], ACT.Abs_reciprocal_sqrt, bias=0.25)
 
         z_words = tile("z_words", [P, S], U32)
         z_scales = tile("z_scales", [P, S], U8)
@@ -214,12 +219,7 @@ def tile_picked_triopullbtriebstd_none_po_kernel(
             for t in range(PACK):
                 nc.vector.tensor_tensor(m_sum[:, t, :], win_m[t][:].indirect(l3[:, entries]), m_again[:, t, cols], ADD)
             z = tile("z%d" % half, [P, PACK * HALF], BF16)
-            if half == 0:
-                z_tiles = tile("z_tiles", [P, PACK, HALF], BF16)
-                nc.vector.tensor_tensor(z_tiles[:], m_sum[:], gate_2[:, :, cols], MULT)
-                nc.scalar.copy(by_word(z[:]), by_tile(z_tiles[:]))
-            else:
-                nc.vector.tensor_tensor(by_word(z[:]), by_tile(m_sum[:]), by_tile(gate_2[:, :, cols]), MULT)
+            nc.vector.tensor_tensor(by_word(z[:]), by_tile(m_sum[:]), by_tile(gate_2[:, :, cols]), MULT)
             nc.vector.quantize_mx(z_words[:, cols].bitcast(FP8X4), z_scales[:, cols], z[:])
             for t0 in range(0, PACK, PAIR):
                 acc = psum.tile([P, BANK], F32, name="bank")
@@ -228,12 +228,21 @@ def tile_picked_triopullbtriebstd_none_po_kernel(
                 for j in range(PAIR):
                     nc.scalar.copy(win_h[t0 + j][:, cols], acc[:, j * HALF : (j + 1) * HALF])
                 h_banks.append(acc)
-        h_part = tile("h_part", [P, UNITS, BANK])
+        h_less = tile("h_less", [P, UNITS, BANK])
+        h_more = tile("h_more", [P, UNITS, BANK])
         for u in range(UNITS):
-            nc.scalar.activation(h_part[:, u, :], h_banks[u][:], ACT.Copy, scale=H_PART)
-        totals = [held.tile([P, BANK], F32, name="held_bank") for u in range(TURNED_UNITS)]
+            nc.scalar.activation(h_less[:, u, :], h_banks[u][:], ACT.Copy, scale=H_LESS)
+            nc.scalar.activation(h_more[:, u, :], h_banks[u][:], ACT.Copy, scale=H_MORE)
+
+        def opened(u, term):
+            acc = held.tile([P, BANK], F32, name="held_bank") if u < PAIR else psum.tile([P, BANK], F32, name="bank")
+            turn(acc, [term], True, False)
+            return acc
+
+        gaps, totals = [], []
         for u in range(TURNED_UNITS):
-            turn(totals[u], [h_part[:, u, :]], True, False)
+            gaps.append(opened(u, h_less[:, u, :]))
+            totals.append(opened(u, h_more[:, u, :]))
 
         o_words = tile("o_words", [P, S], I32)
         o_scales = tile("o_scales", [P, S], U8)
@@ -246,33 +255,32 @@ def tile_picked_triopullbtriebstd_none_po_kernel(
         def spread(u):
             half, t0 = u // PAIR, PAIR * (u % PAIR)
             entries = slice(HALF * half // LIST_COL, HALF * (half + 1) // LIST_COL)
-            neg_pa = tile("neg_pa%d" % u, [P, BANK])
-            q = tile("q%d" % u, [P, BANK])
+            first = tile("first%d" % u, [P, BANK])
+            second = tile("second%d" % u, [P, BANK])
             for j in range(PAIR):
                 own = slice(j * HALF, (j + 1) * HALF)
-                nc.vector.tensor_scalar(neg_pa[:, own], win_h[t0 + j][:].indirect(l5[:, entries]), -1.0, 0.0, MULT, ADD)
+                nc.vector.tensor_tensor(first[:, own], win_h[t0 + j][:].indirect(l5[:, entries]), h_less[:, u, own], ADD)
             for j in range(PAIR):
                 own = slice(j * HALF, (j + 1) * HALF)
-                nc.vector.tensor_tensor(q[:, own], win_h[t0 + j][:].indirect(l6[:, entries]), neg_pa[:, own], SUB)
+                nc.vector.tensor_tensor(second[:, own], win_h[t0 + j][:].indirect(l6[:, entries]), first[:, own], SUB)
+            nc.vector.scalar_tensor_tensor(centred[u][:], first[:], 2.0, second[:], MULT, ADD)
             if u < TURNED_UNITS:
                 sq_gap = tile("sq_gap%d" % u, [P, BANK], F32, "b_sum%d" % u)
                 sq_total = tile("sq_total%d" % u, [P, BANK], F32, "moved%d" % u)
-                nc.vector.scalar_tensor_tensor(centred[u][:], h_part[:, u, :], -2.2 / H_PART, q[:], MULT, ADD)
-                gap = turned_sum([neg_pa[:], neg_pa[:], q[:]])
-                nc.scalar.activation(sq_gap[:], gap[:], ACT.Square, scale=ROOT_HALF)
+                turn(gaps[u], [second[:]], False, True)
+                nc.scalar.activation(sq_gap[:], gaps[u][:], ACT.Square, scale=ROOT_HALF)
                 turn(totals[u], [centred[u][:]], False, True)
                 nc.scalar.activation(sq_total[:], totals[u][:], ACT.Square, scale=0.375 * ROOT_HALF)
                 squares = turned_sum([sq_gap[:], sq_total[:]])
             else:
                 sq_both = tile("sq_both", [P, 2, BANK], F32, "moved1")
-                gap = tile("gap", [P, BANK])
-                total = tile("total", [P, BANK])
-                squares = tile("squares", [P, BANK])
-                nc.vector.scalar_tensor_tensor(gap[:], neg_pa[:], 2.0, q[:], MULT, ADD)
+                gap = tile("gap", [P, BANK], F32, "pulled0")
+                total = tile("total", [P, BANK], F32, "pulled1")
+                squares = tile("squares", [P, BANK], F32, "pulled2")
+                nc.vector.tensor_tensor(gap[:], second[:], h_less[:, u, :], ADD)
                 nc.scalar.activation(sq_both[:, 0, :], gap[:], ACT.Square, scale=ROOT_HALF)
-                nc.vector.scalar_tensor_tensor(total[:], h_part[:, u, :], -5.0 / 3.0 / H_PART, q[:], MULT, ADD)
+                nc.vector.tensor_tensor(total[:], centred[u][:], h_more[:, u, :], ADD)
                 nc.scalar.activation(sq_both[:, 1, :], total[:], ACT.Square, scale=0.375 * ROOT_HALF)
-                nc.vector.scalar_tensor_tensor(centred[u][:], h_part[:, u, :], -2.2 / H_PART, q[:], MULT, ADD)
                 nc.vector.tensor_tensor(squares[:], sq_both[:, 1, :], sq_both[:, 0, :], ADD)
             nc.scalar.activation(inv_root[u][:], squares[:], ACT.Abs_reciprocal_sqrt, bias=0.25)
 

from contextlib import ExitStack

import concourse.mybir as mybir
from concourse.masks import make_identity

K, T, S, N, H = 512, 2048, 512, 512, 512
FLOPS = 2 * S * (3 * K * H + H * N)

F32 = mybir.dt.float32
BF16 = mybir.dt.bfloat16
I32 = mybir.dt.int32
U32 = mybir.dt.uint32
U16 = mybir.dt.uint16
U8 = mybir.dt.uint8
FP8X4 = mybir.dt.float8_e4m3fn_x4
ADD = mybir.AluOpType.add
SUB = mybir.AluOpType.subtract
MULT = mybir.AluOpType.mult
ACT = mybir.ActivationFunctionType

P = 128
PACK = 4
QUADRANTS = 4
BANK = 512
LIST_COL = 16
LINE = 16
HALF = S // 2
PAIR = BANK // HALF
UNITS = S * PACK // BANK
TURNED_UNITS = UNITS - 1
W4_ROWS = 4
H_LESS = -11.0 / 5.0
H_MORE = 8.0 / 15.0
ROOT_HALF = 0.5**0.5


def tile_picked_triopullbtriebstd_none_po_kernel(
    tc, x_words, x_scales, w1_words, w1_scales, w2_words, w2_scales, w3_words, w3_scales, gn, w4_words, w4_scales,
    offs, two, three, n1, n2, n3, n4, n5, n6, out_0, out_1, out_2,
):
    nc = tc.nc
    with ExitStack() as ctx:
        lists = ctx.enter_context(tc.tile_pool(name="lists", bufs=1))
        sb = ctx.enter_context(tc.tile_pool(name="sb", bufs=1))
        psum = ctx.enter_context(tc.psum_pool(name="psum", bufs=4))
        held = ctx.enter_context(tc.psum_pool(name="held", bufs=4))

        def tile(name, shape, dtype=F32, after=""):
            return sb.tile(shape, dtype, name=name, tag=after or name, align_bytes=64)

        def load_list(name, src):
            dst = lists.tile([P, S // LIST_COL], U16, name=name)
            nc.sync.dma_start(dst[:], src)
            return dst

        def load_words(name, src, width):
            dst = tile(name, [P, width], I32)
            nc.sync.dma_start(dst[:], src[0].rearrange("p n t -> p (n t)").bitcast(I32))
            return dst

        def zeroed_plane(name, width, engine):
            dst = tile(name, [P, width], U8)
            engine.memset(dst[:].bitcast(I32), 0)
            return dst

        def load_scales(plane, first, src):
            for q in range(QUADRANTS):
                rows = slice(32 * q + first, 32 * q + first + 4)
                nc.sync.dma_start(plane[rows, :].bitcast(I32), src[0, 4 * q : 4 * q + 4, :].bitcast(I32))

        def deal(name, src, dtype, item_size):
            dst = tile(name, [P, H], dtype)
            run = LINE // item_size
            nc.vector.tensor_copy(
                dst[:].rearrange("p (t c i) -> p c t i", t=PACK, i=run), src[:].rearrange("p (c i t) -> p c t i", t=PACK, i=run)
            )
            return dst

        def pick_words(name, offsets, after=""):
            words = tile(name, [P, S], U32, after)
            nc.vector.tensor_copy(words[:], xw[:].bitcast(U32).indirect(offsets[:]))
            return words

        def pick_scales(name, offsets):
            scales = tile(name, [P, S], U8)
            nc.vector.tensor_copy(scales[:], xs[:].indirect(offsets[:]))
            return scales

        def product(dst, weights, plane, first, t, words, scales):
            cols = slice(P * t, P * (t + 1))
            nc.tensor.matmul_mx(
                dst, lhsT=weights[:, cols].bitcast(FP8X4), lhsT_scale=plane[first:P, cols],
                rhs=words.bitcast(FP8X4), rhs_scale=scales, start=True, stop=True,
            )

        def by_tile(ap):
            return ap.rearrange("p t (c i) -> p c t i", i=4)

        def by_word(ap):
            return ap.rearrange("p (c i t) -> p c t i", i=4, t=PACK)

        def turn(acc, terms, opens, closes):
            blocks = [(term, slice(P * j, P * (j + 1))) for term in terms for j in range(BANK // P)]
            for n, (term, block) in enumerate(blocks):
                nc.tensor.matmul(
                    acc[:, block], lhsT=term[:, block], rhs=ident[:], is_transpose=True,
                    start=(opens and n == 0), stop=(closes and n == len(blocks) - 1),
                )

        def turned_sum(terms):
            acc = psum.tile([P, BANK], F32, name="bank")
            turn(acc, terms, True, True)
            return acc

        xs = zeroed_plane("xs", T, nc.vector)
        plane_w2 = zeroed_plane("plane_w2", H, nc.gpsimd)
        plane_w34 = zeroed_plane("plane_w34", H, nc.gpsimd)
        plane_w1 = zeroed_plane("plane_w1", H, nc.gpsimd)
        warm = tile("warm", [P, 2])
        nc.vector.memset(warm[:, 0:1], 1.0)
        nc.scalar.activation(warm[:, 1:2], warm[:, 0:1], ACT.Sigmoid)
        l_two = load_list("l_two", two)
        l_offs = load_list("l_offs", offs)
        l_three = load_list("l_three", three)
        load_scales(xs, 0, x_scales)
        gain = tile("gain", [P, PACK])
        nc.sync.dma_start(gain[:], gn.rearrange("(p t) o -> p (t o)", t=PACK))
        xw = load_words("xw", x_words, T)
        w2_raw = load_words("w2_raw", w2_words, H)
        load_scales(plane_w2, 0, w2_scales)
        w1_raw = load_words("w1_raw", w1_words, H)
        l2 = load_list("l2", n2)
        load_scales(plane_w1, 0, w1_scales)
        l1 = load_list("l1", n1)
        load_scales(plane_w34, 0, w3_scales)
        load_scales(plane_w34, W4_ROWS, w4_scales)
        l4 = load_list("l4", n4)
        w3_raw = load_words("w3_raw", w3_words, H)
        l3 = load_list("l3", n3)
        w4_raw = load_words("w4_raw", w4_words, N)
        l5 = load_list("l5", n5)
        l6 = load_list("l6", n6)
        ident = tile("ident", [P, P])
        make_identity(nc, ident[:])

        low, high = slice(0, S), slice(S, 2 * S)
        win_d = [tile("win_d%d" % t, [P, 2 * S]) for t in range(PACK)]
        win_y = [tile("win_y%d" % t, [P, 2 * S]) for t in range(PACK)]
        win_b = [tile("win_b%d" % t, [P, 2 * S]) for t in range(PACK)]
        gate_2 = tile("gate_2", [P, PACK, S])
        win_m = [tile("win_m%d" % t, [P, S]) for t in range(PACK)]
        y_again = tile("y_again", [P, PACK, S])
        m_again = tile("m_again", [P, PACK, S])

        def project(window, again, weights, plane, words, scales, t, factor, by_dma):
            acc = psum.tile([P, BANK], F32, name="bank")
            product(acc[:], weights, plane, 0, t, words[:], scales[:])
            if not by_dma:
                nc.scalar.activation(again, acc[:], ACT.Copy, scale=factor)
            nc.scalar.activation(window, acc[:], ACT.Copy, scale=factor)
            if by_dma:
                nc.sync.dma_start(again, window)

        def mix(t):
            pulled = tile("pulled%d" % t, [P, S])
            nc.vector.tensor_tensor(pulled[:], win_y[t][:].indirect(l1[:]), y_again[:, t, :], SUB)
            moved = tile("moved%d" % t, [P, S])
            acc = held.tile([P, BANK], F32, name="held_bank")
            turn(acc, [win_y[t][:, low]], True, False)
            nc.vector.tensor_tensor(moved[:], pulled[:], gate_1[:, t, :], MULT)
            turn(acc, [moved[:]], False, True)
            nc.scalar.copy(gate_2[:, t, :], acc[:])
            back = turned_sum([gate_2[:, t, :]])
            nc.scalar.copy(win_m[t][:], back[:])
            if t < PACK // 2:
                nc.sync.dma_start(m_again[:, t, :], win_m[t][:])
            else:
                nc.scalar.copy(m_again[:, t, :], back[:])

        two_scales = pick_scales("two_scales", l_two)
        offs_scales = pick_scales("offs_scales", l_offs)
        three_scales = pick_scales("three_scales", l_three)
        two_words = pick_words("two_words", l_two)
        w2 = deal("w2", w2_raw, I32, 4)
        scales_w2 = deal("scales_w2", plane_w2, U8, 1)
        for t in range(PACK):
            project(win_d[t][:, low], win_d[t ^ 1][:, high], w2, scales_w2, two_words, two_scales, t, 1.0, False)
        offs_words = pick_words("offs_words", l_offs, "plane_w2")
        w1 = deal("w1", w1_raw, I32, 4)
        scales_w1 = deal("scales_w1", plane_w1, U8, 1)
        for t in range(PACK):
            project(win_y[t][:, low], y_again[:, t, :], w1, scales_w1, offs_words, offs_scales, t, gain[:, t : t + 1], t > 0)
        three_words = pick_words("three_words", l_three, "w1_raw")
        gate_1 = tile("gate_1", [P, PACK, S], F32, "plane_w2")
        w3 = deal("w3", w3_raw, I32, 4)
        scales_w34 = deal("scales_w34", plane_w34, U8, 1)
        for t in range(PACK):
            nc.vector.tensor_tensor(win_y[t][:, high], win_d[t][:].indirect(l2[:]), win_d[t ^ 1][:, high], SUB)
            nc.scalar.activation(gate_1[:, t, :], win_y[t][:, high], ACT.Sigmoid)
        for t in range(PACK):
            project(win_b[t][:, low], win_b[t ^ 1][:, high], w3, scales_w34, three_words, three_scales, t, 1.0, True)
        w4 = deal("w4", w4_raw, I32, 4)
        for t in range(PACK):
            mix(t)
        for t in range(PACK):
            b_sum = tile("b_sum%d" % t, [P, S])
            nc.vector.tensor_tensor(b_sum[:], win_b[t][:].indirect(l4[:]), win_b[t ^ 1][:, high], ADD)
            nc.scalar.activation(gate_2[:, t, :], b_sum[:], ACT.Sigmoid)
        nc.scalar.activation(warm[:, 1:2], gate_2[:, PACK - 1, 0:1], ACT.Abs_reciprocal_sqrt, bias=0.25)

        z_words = tile("z_words", [P, S], U32)
        z_scales = tile("z_scales", [P, S], U8)
        win_h = [tile("win_h%d" % t, [P, S]) for t in range(PACK)]
        h_banks = []
        for half in range(2):
            cols = slice(HALF * half, HALF * (half + 1))
            entries = slice(cols.start // LIST_COL, cols.stop // LIST_COL)
            m_sum = tile("m_sum%d" % half, [P, PACK, HALF], F32, "m_sum")
            for t in range(PACK):
                nc.vector.tensor_tensor(m_sum[:, t, :], win_m[t][:].indirect(l3[:, entries]), m_again[:, t, cols], ADD)
            z = tile("z%d" % half, [P, PACK * HALF], BF16)
            nc.vector.tensor_tensor(by_word(z[:]), by_tile(m_sum[:]), by_tile(gate_2[:, :, cols]), MULT)
            nc.vector.quantize_mx(z_words[:, cols].bitcast(FP8X4), z_scales[:, cols], z[:])
            for t0 in range(0, PACK, PAIR):
                acc = psum.tile([P, BANK], F32, name="bank")
                for j in range(PAIR):
                    product(acc[:, j * HALF : (j + 1) * HALF], w4, scales_w34, W4_ROWS, t0 + j, z_words[:, cols], z_scales[:, cols])
                for j in range(PAIR):
                    nc.scalar.copy(win_h[t0 + j][:, cols], acc[:, j * HALF : (j + 1) * HALF])
                h_banks.append(acc)
        h_less = tile("h_less", [P, UNITS, BANK])
        h_more = tile("h_more", [P, UNITS, BANK])
        for u in range(UNITS):
            nc.scalar.activation(h_less[:, u, :], h_banks[u][:], ACT.Copy, scale=H_LESS)
            nc.scalar.activation(h_more[:, u, :], h_banks[u][:], ACT.Copy, scale=H_MORE)

        def opened(u, term):
            acc = held.tile([P, BANK], F32, name="held_bank") if u < PAIR else psum.tile([P, BANK], F32, name="bank")
            turn(acc, [term], True, False)
            return acc

        gaps, totals = [], []
        for u in range(TURNED_UNITS):
            gaps.append(opened(u, h_less[:, u, :]))
            totals.append(opened(u, h_more[:, u, :]))

        o_words = tile("o_words", [P, S], I32)
        o_scales = tile("o_scales", [P, S], U8)
        out_rows = out_0.rearrange("(p t) c -> p t c", t=PACK)
        out_words = out_1[0].rearrange("p n t -> p (n t)").bitcast(I32)
        inv_root = [tile("inv_root%d" % u, [P, BANK]) for u in range(UNITS)]
        centred = [tile("centred%d" % u, [P, BANK]) for u in range(UNITS)]
        result = tile("result", [P, UNITS, BANK])

        def spread(u):
            half, t0 = u // PAIR, PAIR * (u % PAIR)
            entries = slice(HALF * half // LIST_COL, HALF * (half + 1) // LIST_COL)
            first = tile("first%d" % u, [P, BANK])
            second = tile("second%d" % u, [P, BANK])
            for j in range(PAIR):
                own = slice(j * HALF, (j + 1) * HALF)
                nc.vector.tensor_tensor(first[:, own], win_h[t0 + j][:].indirect(l5[:, entries]), h_less[:, u, own], ADD)
            for j in range(PAIR):
                own = slice(j * HALF, (j + 1) * HALF)
                nc.vector.tensor_tensor(second[:, own], win_h[t0 + j][:].indirect(l6[:, entries]), first[:, own], SUB)
            nc.vector.scalar_tensor_tensor(centred[u][:], first[:], 2.0, second[:], MULT, ADD)
            if u < TURNED_UNITS:
                sq_gap = tile("sq_gap%d" % u, [P, BANK], F32, "b_sum%d" % u)
                sq_total = tile("sq_total%d" % u, [P, BANK], F32, "moved%d" % u)
                turn(gaps[u], [second[:]], False, True)
                nc.scalar.activation(sq_gap[:], gaps[u][:], ACT.Square, scale=ROOT_HALF)
                turn(totals[u], [centred[u][:]], False, True)
                nc.scalar.activation(sq_total[:], totals[u][:], ACT.Square, scale=0.375 * ROOT_HALF)
                squares = turned_sum([sq_gap[:], sq_total[:]])
            else:
                sq_both = tile("sq_both", [P, 2, BANK], F32, "moved1")
                gap = tile("gap", [P, BANK], F32, "pulled0")
                total = tile("total", [P, BANK], F32, "pulled1")
                squares = tile("squares", [P, BANK], F32, "pulled2")
                nc.vector.tensor_tensor(gap[:], second[:], h_less[:, u, :], ADD)
                nc.scalar.activation(sq_both[:, 0, :], gap[:], ACT.Square, scale=ROOT_HALF)
                nc.vector.tensor_tensor(total[:], centred[u][:], h_more[:, u, :], ADD)
                nc.scalar.activation(sq_both[:, 1, :], total[:], ACT.Square, scale=0.375 * ROOT_HALF)
                nc.vector.tensor_tensor(squares[:], sq_both[:, 1, :], sq_both[:, 0, :], ADD)
            nc.scalar.activation(inv_root[u][:], squares[:], ACT.Abs_reciprocal_sqrt, bias=0.25)

        def finish(u):
            nc.vector.scalar_tensor_tensor(result[:, u, :], centred[u][:], -0.3125, inv_root[u][:], MULT, MULT)
            if u % PAIR == PAIR - 1:
                half = u // PAIR
                cols = slice(HALF * half, HALF * (half + 1))
                tiles = result[:, PAIR * half : PAIR * (half + 1), :].rearrange("p u (j c) -> p (u j) c", j=PAIR)
                nc.sync.dma_start(out_rows[:, :, cols], tiles)
                rounded = tile("rounded%d" % half, [P, PACK * HALF], BF16)
                nc.vector.tensor_copy(by_word(rounded[:]), by_tile(tiles))
                nc.vector.quantize_mx(o_words[:, cols].bitcast(FP8X4), o_scales[:, cols], rounded[:])
                nc.sync.dma_start(out_words[:, cols], o_words[:, cols])

        spread(0)
        for u in range(1, UNITS):
            spread(u)
            finish(u - 1)
        finish(UNITS - 1)
        for r in range(QUADRANTS):
            queue = (nc.scalar, nc.sync)[r % 2]
            queue.dma_start(out_2[0, 4 * r : 4 * r + 4, :].bitcast(I32), o_scales[32 * r : 32 * r + 4, :].bitcast(I32))
